import numpy as np
import ml_dtypes


def mxq(x, axis, fmt="e4m3"):
    dtype, down = {"e4m3": (ml_dtypes.float8_e4m3fn, 7), "e5m2": (ml_dtypes.float8_e5m2, 14)}[fmt]
    v = np.moveaxis(np.asarray(x, np.float32).astype(ml_dtypes.bfloat16).astype(np.float64), axis, -1)
    blocks = v.reshape(v.shape[:-1] + (-1, 32))
    amax = np.abs(blocks).max(-1, keepdims=True)
    byte = np.maximum(np.where(amax > 0, np.frexp(amax)[1] - 1 + 127, 0) - down, 1)
    scale = np.exp2(byte - 127.0)
    codes = (blocks / scale).astype(np.float32).astype(dtype).astype(np.float64)
    return np.moveaxis((codes * scale).reshape(v.shape), -1, axis)


WIDE = False


def mx_kscale(k):
    if not WIDE:
        return np.ones(k)
    levels = np.array([10, -10, 5, -5, 0])
    if k % 512:
        return np.exp2(np.random.permutation(np.resize(levels, k // 32))).repeat(32)
    a = np.empty((k // 512, 16))
    for p in range(k // 512):
        a[p, :8] = np.random.permutation(np.resize(levels, 8))
        for g in range(8):
            far = levels[np.abs(levels - a[p, g]) >= 10]
            a[p, g + 8] = far[np.random.randint(len(far))]
    return np.exp2(a.ravel()).repeat(32)


def f64(x):
    return np.asarray(x).astype(np.float64)


def striped(idx):
    return np.tile(np.asarray(idx).reshape(-1, 16).T, (8, 1)).astype(np.uint16)


def unstriped(offs):
    return offs[:16].T.reshape(-1).astype(np.int64)


E2M1 = np.array([0.0, 0.5, 1.0, 1.5, 2.0, 3.0, 4.0, 6.0, -0.0, -0.5, -1.0, -1.5, -2.0, -3.0, -4.0, -6.0])


def pack_weight(w, fmt):
    k, n = w.shape
    w = f64(np.asarray(w, np.float32).astype(ml_dtypes.bfloat16)).reshape(k // 32, 32, n)
    amax = np.abs(w).max(1)
    if fmt == "e4m3":
        byte = np.frexp(amax)[1] - 1 + 127 - 7
    else:
        mant, ex = np.frexp(amax / 6.0)
        byte = np.where(mant > 0.5, ex, ex - 1) + 127
    byte = np.clip(np.where(amax > 0, byte, 1), 1, 254)
    scaled = (w * np.exp2(127.0 - byte)[:, None, :]).reshape(k, n).astype(np.float32)
    by_word = np.ascontiguousarray(scaled.reshape(k // 512, 128, 4, n).transpose(0, 1, 3, 2))
    if fmt == "e4m3":
        words = by_word.astype(ml_dtypes.float8_e4m3fn).view(np.uint8)
    else:
        c = by_word.astype(ml_dtypes.float4_e2m1fn).view(np.uint8) & 0xF
        words = (c[..., 0::2] | (c[..., 1::2] << 4)).reshape(k // 512, 128, 2 * n)
    return np.ascontiguousarray(words), np.ascontiguousarray(byte.astype(np.uint8).reshape(k // 512, 16, n))


def unpack_weight(words, scales, fmt):
    g, _, n = scales.shape
    words = np.ascontiguousarray(words).reshape(g, 128, n, -1)
    if fmt == "e4m3":
        vals = words.view(ml_dtypes.float8_e4m3fn).astype(np.float64)
    else:
        nib = np.empty((g, 128, n, 4), np.uint8)
        nib[..., 0::2] = words & 0xF
        nib[..., 1::2] = words >> 4
        vals = E2M1[nib]
    vals = vals * np.repeat(np.exp2(scales.astype(np.float64) - 127.0), 8, axis=1)[..., None]
    return vals.transpose(0, 1, 3, 2).reshape(g * 512, n)


def softplus(v):
    return np.log(1.0 + np.exp(v))


def sigmoid(v):
    return 1.0 / (1.0 + np.exp(-v))


D, T, U, I, J, G = 512, 1024, 1024, 256, 512, 128


def setup_inputs():
    n = np.random.standard_normal
    idx = np.random.permutation(T)[:I]
    idx2 = np.random.permutation(U)[:J]
    fd = mx_kscale(D)
    tabbp = pack_weight(n((D, U)) / fd[:, None], "e4m3")
    return {
        "taba": (n((D, T)) * 1 / np.sqrt(D) * fd[:, None]).astype(np.float32),
        "tabb_words": tabbp[0],
        "tabb_scales": tabbp[1],
        "stake": (n((I, G)) * 4.0).astype(np.float32),
        "bias": (np.random.uniform(0.0, 2.0, (1, J))).astype(np.float32),
        "old": (0.3 * n((I, J))).astype(np.float32),
        "offs": striped(idx),
        "offs2": striped(idx2),
    }


def reference(taba, tabb_words, tabb_scales, stake, bias, old, offs, offs2):
    idx = unstriped(offs)
    idx2 = unstriped(offs2)
    tabbu = unpack_weight(tabb_words, tabb_scales, "e4m3")
    tabaidxq = mxq(f64(taba)[:, idx], 0, "e4m3")
    tabbidx2g = tabbu[:, idx2]
    s = tabaidxq.T @ tabbidx2g
    u1 = softplus((s + f64(bias)) * (-1.0))
    ch = np.exp(u1.reshape(I, G, J // G).sum(axis=2) * (-1.0))
    dch = f64(stake) / (ch + 1.0)
    e1 = dch * ch * (-1.0)
    r1 = np.repeat(e1, J // G, axis=1)
    ds = r1 * sigmoid((s + f64(bias)) * (-1.0)) * (-1.0)
    y = ds + f64(old)
    return y

@@ -1,0 +1,155 @@
+from contextlib import ExitStack
+
+import concourse.mybir as mybir
+from concourse.masks import make_identity
+
+D, T, U, I, J, G = 512, 1024, 1024, 256, 512, 128
+FLOPS = 2 * D * I * J
+
+F32 = mybir.dt.float32
+BF16 = mybir.dt.bfloat16
+I32 = mybir.dt.int32
+U32 = mybir.dt.uint32
+U16 = mybir.dt.uint16
+U8 = mybir.dt.uint8
+FP8X4 = mybir.dt.float8_e4m3fn_x4
+ALU = mybir.AluOpType
+ACT = mybir.ActivationFunctionType
+
+P = 128
+PACK = 4
+TEAM = J // G
+BLOCKS = I // P
+HALF = P // 2
+
+
+def tile_attend_bpairteams_kernel(tc, taba, tabb_words, tabb_scales, stake, bias, old, offs, offs2, out):
+    nc = tc.nc
+    with ExitStack() as ctx:
+        keep = ctx.enter_context(tc.tile_pool(name="keep", bufs=1))
+        psum = ctx.enter_context(tc.psum_pool(name="psum", bufs=1))
+
+        offs2_sb = keep.tile([P, J // 16], U16, name="offs2_sb")
+        nc.sync.dma_start(offs2_sb[:], offs2)
+        b_word_table = keep.tile([P, U], I32, name="b_word_table", align_bytes=64)
+        nc.sync.dma_start(b_word_table[:], tabb_words[0].rearrange("p n t -> p (n t)").bitcast(I32))
+        offs_sb = keep.tile([P, I // 16], U16, name="offs_sb")
+        nc.sync.dma_start(offs_sb[:], offs)
+
+        b_scale_table = keep.tile([P, U], U8, name="b_scale_table", align_bytes=64)
+        for q in range(4):
+            rows = tabb_scales[0, 4 * q : 4 * q + 4, :].bitcast(I32)
+            nc.scalar.dma_start(
+                b_scale_table[32 * q : 32 * q + 32, :].bitcast(I32),
+                rows.unsqueeze(0).to_broadcast([8, 4, U // 4]),
+            )
+
+        a_rows = taba.rearrange("(p t) n -> p t n", t=PACK)
+        first = keep.tile([P, 2, T], F32, name="a_first", align_bytes=64)
+        nc.sync.dma_start(first[:], a_rows[:, 0:2, :])
+        a_planes = [first[:, 0, :], first[:, 1, :]]
+        for t in range(2, PACK):
+            plane = keep.tile([P, T], F32, name=f"a_plane{t}", align_bytes=64)
+            nc.sync.dma_start(plane[:], a_rows[:, t, :])
+            a_planes.append(plane[:])
+
+        bias_sb = keep.tile([P, TEAM], F32, name="bias_sb")
+        nc.scalar.dma_start(bias_sb[:], bias.rearrange("o (g r) -> (o g) r", r=TEAM))
+        stake_sb = keep.tile([P, BLOCKS, G], F32, name="stake_sb")
+        nc.sync.dma_start(stake_sb[:], stake.rearrange("(b p) g -> p b g", p=P))
+        old_sb = []
+        for b in range(BLOCKS):
+            o = keep.tile([P, J], F32, name=f"old{b}")
+            nc.sync.dma_start(o[:], old[b * P : (b + 1) * P, :])
+            old_sb.append(o)
+
+        ident = keep.tile([P, P], F32, name="ident")
+        make_identity(nc, ident[:])
+
+        b_scales_listed = keep.tile([P, J], U8, name="b_scales_listed", align_bytes=64)
+        nc.vector.tensor_copy(b_scales_listed[:], b_scale_table[:].indirect(offs2_sb[:]))
+        b_words = keep.tile([P, J], U32, name="b_words", align_bytes=64)
+        nc.vector.tensor_copy(
+            b_words[:].rearrange("p (r g) -> p g r", r=TEAM),
+            b_word_table[:].bitcast(U32).indirect(offs2_sb[:]),
+        )
+        b_scales = keep.tile([P, J], U8, name="b_scales", align_bytes=64)
+        nc.vector.tensor_copy(
+            b_scales[:].rearrange("p (r g) -> p g r", r=TEAM),
+            b_scales_listed[:].rearrange("p (g r) -> p g r", r=TEAM),
+        )
+
+        cols = P // 16
+        both = range(BLOCKS)
+        grouped = keep.tile([P, I, PACK], BF16, name="grouped", align_bytes=64)
+        for t in range(PACK - 1):
+            nc.vector.tensor_copy(grouped[:, :, t], a_planes[t].indirect(offs_sb[:]))
+        for b in both:
+            nc.vector.tensor_copy(
+                grouped[:, b * P : (b + 1) * P, PACK - 1], a_planes[PACK - 1].indirect(offs_sb[:, b * cols : (b + 1) * cols])
+            )
+        a_words, a_scales = [], []
+        for b in both:
+            w = keep.tile([P, P], U32, name=f"a_words{b}", align_bytes=64)
+            s = keep.tile([P, P], U8, name=f"a_scales{b}", align_bytes=64)
+            nc.vector.quantize_mx(
+                out=w[:].bitcast(FP8X4), scales=s[:], in_=grouped[:, b * P : (b + 1) * P, :].rearrange("p n t -> p (n t)")
+            )
+            a_words.append(w)
+            a_scales.append(s)
+
+        scores = {}
+        for b in both:
+            for h in range(2):
+                bank = psum.tile([P, 2, P], F32, name=f"scores{b}{h}")
+                for e in range(2):
+                    r = 2 * h + e
+                    nc.tensor.matmul_mx(
+                        out=bank[:, e, :],
+                        lhsT=b_words[:, r * G : (r + 1) * G].bitcast(FP8X4),
+                        lhsT_scale=b_scales[:, r * G : (r + 1) * G],
+                        rhs=a_words[b][:].bitcast(FP8X4),
+                        rhs_scale=a_scales[b][:],
+                        start=True,
+                        stop=True,
+                    )
+                    scores[b, r] = bank[:, e, :]
+
+        def tiles(name, shape):
+            return [keep.tile(shape, F32, name=f"{name}{b}") for b in both]
+
+        win = tiles("win", [P, TEAM, P])
+        turned = []
+        for b in both:
+            for r in range(TEAM):
+                nc.scalar.activation(win[b][:, r, :], scores[b, r], ACT.Sigmoid, bias=bias_sb[:, r : r + 1], scale=1.0)
+        for b in both:
+            bank = psum.tile([P, TEAM, G], F32, name=f"turned{b}")
+            for r in range(TEAM):
+                nc.tensor.transpose(bank[:, r, :], win[b][:, r, :], ident[:])
+            turned.append(bank[:].rearrange("p r g -> p g r"))
+
+        chance = tiles("chance", [P, G])
+        staked = tiles("staked", [P, G])
+        root = tiles("root", [P, G])
+        inv = tiles("inv", [P, G])
+        coef = tiles("coef", [P, G])
+        grad = tiles("grad", [P, G, TEAM])
+        res = tiles("res", [P, J])
+        for b in both:
+            nc.vector.tensor_reduce(chance[b][:], turned[b], mybir.AxisListType.X, ALU.mult)
+        for b in both:
+            nc.vector.tensor_tensor(staked[b][:], chance[b][:], stake_sb[:, b, :], ALU.mult)
+        for b in both:
+            nc.scalar.activation(root[b][:], chance[b][:], ACT.Abs_reciprocal_sqrt, bias=1.0, scale=1.0)
+        for b in both:
+            nc.scalar.activation(inv[b][:], root[b][:], ACT.Square)
+        for b in both:
+            nc.vector.tensor_tensor(coef[b][:], staked[b][:], inv[b][:], ALU.mult)
+        for b in both:
+            nc.vector.scalar_tensor_tensor(
+                grad[b][:], turned[b], 1.0, coef[b][:].unsqueeze(2).to_broadcast([P, G, TEAM]), ALU.subtract, ALU.mult
+            )
+        for b in both:
+            nc.vector.tensor_tensor(res[b][:], old_sb[b][:], grad[b][:].rearrange("p g r -> p (g r)"), ALU.subtract)
+            nc.sync.dma_start(out[b * P : (b + 1) * P, :], res[b][:])

@@ -20,7 +20,7 @@ P = 128
 PACK = 4
 TEAM = J // G
 BLOCKS = I // P
-HALF = P // 2
+JB = J // P
 
 
 def tile_attend_bpairteams_kernel(tc, taba, tabb_words, tabb_scales, stake, bias, old, offs, offs2, out):
@@ -29,10 +29,13 @@ def tile_attend_bpairteams_kernel(tc, taba, tabb_words, tabb_scales, stake, bias
         keep = ctx.enter_context(tc.tile_pool(name="keep", bufs=1))
         psum = ctx.enter_context(tc.psum_pool(name="psum", bufs=1))
 
+        a_rows = taba.rearrange("(p t) n -> p t n", t=PACK)
+        a_planes = [keep.tile([P, T], F32, name=f"a_plane{t}", align_bytes=64) for t in range(PACK)]
+        both = range(BLOCKS)
+
         offs2_sb = keep.tile([P, J // 16], U16, name="offs2_sb")
         nc.sync.dma_start(offs2_sb[:], offs2)
-        b_word_table = keep.tile([P, U], I32, name="b_word_table", align_bytes=64)
-        nc.sync.dma_start(b_word_table[:], tabb_words[0].rearrange("p n t -> p (n t)").bitcast(I32))
+        nc.sync.dma_start(a_planes[0][:], a_rows[:, 0, :])
         offs_sb = keep.tile([P, I // 16], U16, name="offs_sb")
         nc.sync.dma_start(offs_sb[:], offs)
 
@@ -43,113 +46,103 @@ def tile_attend_bpairteams_kernel(tc, taba, tabb_words, tabb_scales, stake, bias
                 b_scale_table[32 * q : 32 * q + 32, :].bitcast(I32),
                 rows.unsqueeze(0).to_broadcast([8, 4, U // 4]),
             )
+        for t in range(1, PACK):
+            nc.sync.dma_start(a_planes[t][:], a_rows[:, t, :])
+        b_word_table = keep.tile([P, U], I32, name="b_word_table", align_bytes=64)
+        nc.sync.dma_start(b_word_table[:], tabb_words[0].rearrange("p n t -> p (n t)").bitcast(I32))
 
-        a_rows = taba.rearrange("(p t) n -> p t n", t=PACK)
-        first = keep.tile([P, 2, T], F32, name="a_first", align_bytes=64)
-        nc.sync.dma_start(first[:], a_rows[:, 0:2, :])
-        a_planes = [first[:, 0, :], first[:, 1, :]]
-        for t in range(2, PACK):
-            plane = keep.tile([P, T], F32, name=f"a_plane{t}", align_bytes=64)
-            nc.sync.dma_start(plane[:], a_rows[:, t, :])
-            a_planes.append(plane[:])
-
-        bias_sb = keep.tile([P, TEAM], F32, name="bias_sb")
-        nc.scalar.dma_start(bias_sb[:], bias.rearrange("o (g r) -> (o g) r", r=TEAM))
+        bias_rows = keep.tile([P, P], F32, name="bias_rows")
+        nc.gpsimd.memset(bias_rows[:], 0.0)
+        nc.scalar.dma_start(bias_rows[0:JB, :], bias.rearrange("o (c p) -> (o c) p", p=P))
         stake_sb = keep.tile([P, BLOCKS, G], F32, name="stake_sb")
         nc.sync.dma_start(stake_sb[:], stake.rearrange("(b p) g -> p b g", p=P))
         old_sb = []
-        for b in range(BLOCKS):
+        for b in both:
             o = keep.tile([P, J], F32, name=f"old{b}")
             nc.sync.dma_start(o[:], old[b * P : (b + 1) * P, :])
             old_sb.append(o)
 
         ident = keep.tile([P, P], F32, name="ident")
         make_identity(nc, ident[:])
+        bias_turned = psum.tile([P, 2 * P], F32, name="bias_turned", tag="turned11")
+        nc.tensor.transpose(bias_turned[:, 0:P], bias_rows[:], ident[:])
+        bias_sb = keep.tile([P, JB], F32, name="bias_sb")
+        nc.vector.tensor_copy(bias_sb[:], bias_turned[:, 0:JB])
 
-        b_scales_listed = keep.tile([P, J], U8, name="b_scales_listed", align_bytes=64)
-        nc.vector.tensor_copy(b_scales_listed[:], b_scale_table[:].indirect(offs2_sb[:]))
-        b_words = keep.tile([P, J], U32, name="b_words", align_bytes=64)
-        nc.vector.tensor_copy(
-            b_words[:].rearrange("p (r g) -> p g r", r=TEAM),
-            b_word_table[:].bitcast(U32).indirect(offs2_sb[:]),
-        )
         b_scales = keep.tile([P, J], U8, name="b_scales", align_bytes=64)
-        nc.vector.tensor_copy(
-            b_scales[:].rearrange("p (r g) -> p g r", r=TEAM),
-            b_scales_listed[:].rearrange("p (g r) -> p g r", r=TEAM),
-        )
+        nc.vector.tensor_copy(b_scales[:], b_scale_table[:].indirect(offs2_sb[:]))
+
+        grouped = keep.tile([P, I, PACK], BF16, name="grouped", align_bytes=64)
+        for t in range(PACK):
+            nc.vector.tensor_copy(grouped[:, :, t], a_planes[t][:].indirect(offs_sb[:]))
+        a_words = keep.tile([P, I], U32, name="a_words", align_bytes=64)
+        a_scales = keep.tile([P, I], U8, name="a_scales", align_bytes=64)
+        nc.vector.quantize_mx(out=a_words[:].bitcast(FP8X4), scales=a_scales[:], in_=grouped[:].rearrange("p n t -> p (n t)"))
 
         cols = P // 16
-        both = range(BLOCKS)
-        grouped = keep.tile([P, I, PACK], BF16, name="grouped", align_bytes=64)
-        for t in range(PACK - 1):
-            nc.vector.tensor_copy(grouped[:, :, t], a_planes[t].indirect(offs_sb[:]))
-        for b in both:
-            nc.vector.tensor_copy(
-                grouped[:, b * P : (b + 1) * P, PACK - 1], a_planes[PACK - 1].indirect(offs_sb[:, b * cols : (b + 1) * cols])
-            )
-        a_words, a_scales = [], []
-        for b in both:
-            w = keep.tile([P, P], U32, name=f"a_words{b}", align_bytes=64)
-            s = keep.tile([P, P], U8, name=f"a_scales{b}", align_bytes=64)
-            nc.vector.quantize_mx(
-                out=w[:].bitcast(FP8X4), scales=s[:], in_=grouped[:, b * P : (b + 1) * P, :].rearrange("p n t -> p (n t)")
-            )
-            a_words.append(w)
-            a_scales.append(s)
-
-        scores = {}
+        turned = {}
         for b in both:
             for h in range(2):
-                bank = psum.tile([P, 2, P], F32, name=f"scores{b}{h}")
-                for e in range(2):
-                    r = 2 * h + e
-                    nc.tensor.matmul_mx(
-                        out=bank[:, e, :],
-                        lhsT=b_words[:, r * G : (r + 1) * G].bitcast(FP8X4),
-                        lhsT_scale=b_scales[:, r * G : (r + 1) * G],
-                        rhs=a_words[b][:].bitcast(FP8X4),
-                        rhs_scale=a_scales[b][:],
-                        start=True,
-                        stop=True,
-                    )
-                    scores[b, r] = bank[:, e, :]
+                turned[b, h] = psum.tile([P, 2 * P], F32, name=f"turned{b}{h}", tag=f"turned{b}{h}")
+        wins = []
+        for c in range(JB):
+            b_words = keep.tile([P, P], U32, name=f"b_words{c}", align_bytes=64)
+            nc.vector.tensor_copy(b_words[:], b_word_table[:].bitcast(U32).indirect(offs2_sb[:, c * cols : (c + 1) * cols]))
+            scores = psum.tile([P, I], F32, name=f"scores{c}")
+            nc.tensor.matmul_mx(
+                out=scores[:],
+                lhsT=b_words[:].bitcast(FP8X4),
+                lhsT_scale=b_scales[:, c * P : (c + 1) * P],
+                rhs=a_words[:].bitcast(FP8X4),
+                rhs_scale=a_scales[:],
+                start=True,
+                stop=True,
+            )
+            win = keep.tile([P, I], F32, name=f"win{c}")
+            nc.scalar.activation(win[:], scores[:], ACT.Sigmoid, bias=bias_sb[:, c : c + 1], scale=1.0)
+            wins.append(win)
+        for c in range(JB):
+            h, e = divmod(c, 2)
+            for b in both:
+                nc.tensor.transpose(turned[b, h][:, e * P : (e + 1) * P], wins[c][:, b * P : (b + 1) * P], ident[:])
 
         def tiles(name, shape):
             return [keep.tile(shape, F32, name=f"{name}{b}") for b in both]
 
-        win = tiles("win", [P, TEAM, P])
-        turned = []
-        for b in both:
-            for r in range(TEAM):
-                nc.scalar.activation(win[b][:, r, :], scores[b, r], ACT.Sigmoid, bias=bias_sb[:, r : r + 1], scale=1.0)
-        for b in both:
-            bank = psum.tile([P, TEAM, G], F32, name=f"turned{b}")
-            for r in range(TEAM):
-                nc.tensor.transpose(bank[:, r, :], win[b][:, r, :], ident[:])
-            turned.append(bank[:].rearrange("p r g -> p g r"))
-
         chance = tiles("chance", [P, G])
+        squared = tiles("squared", [P, G])
         staked = tiles("staked", [P, G])
-        root = tiles("root", [P, G])
         inv = tiles("inv", [P, G])
         coef = tiles("coef", [P, G])
-        grad = tiles("grad", [P, G, TEAM])
+        grad = tiles("grad", [P, J])
         res = tiles("res", [P, J])
+        GH = G // 2
+        for h in range(2):
+            for b in both:
+                nc.vector.tensor_reduce(
+                    chance[b][:, h * GH : (h + 1) * GH],
+                    turned[b, h][:].rearrange("p (g r) -> p g r", r=TEAM),
+                    mybir.AxisListType.X,
+                    ALU.mult,
+                )
         for b in both:
-            nc.vector.tensor_reduce(chance[b][:], turned[b], mybir.AxisListType.X, ALU.mult)
+            nc.vector.scalar_tensor_tensor(squared[b][:], chance[b][:], 2.0, chance[b][:], ALU.add, ALU.mult)
         for b in both:
             nc.vector.tensor_tensor(staked[b][:], chance[b][:], stake_sb[:, b, :], ALU.mult)
         for b in both:
-            nc.scalar.activation(root[b][:], chance[b][:], ACT.Abs_reciprocal_sqrt, bias=1.0, scale=1.0)
-        for b in both:
-            nc.scalar.activation(inv[b][:], root[b][:], ACT.Square)
+            nc.scalar.activation(inv[b][:], squared[b][:], ACT.Abs_reciprocal_sqrt, bias=1.0, scale=1.0)
         for b in both:
             nc.vector.tensor_tensor(coef[b][:], staked[b][:], inv[b][:], ALU.mult)
         for b in both:
-            nc.vector.scalar_tensor_tensor(
-                grad[b][:], turned[b], 1.0, coef[b][:].unsqueeze(2).to_broadcast([P, G, TEAM]), ALU.subtract, ALU.mult
-            )
-        for b in both:
-            nc.vector.tensor_tensor(res[b][:], old_sb[b][:], grad[b][:].rearrange("p g r -> p (g r)"), ALU.subtract)
-            nc.sync.dma_start(out[b * P : (b + 1) * P, :], res[b][:])
+            for h in range(2):
+                nc.vector.scalar_tensor_tensor(
+                    grad[b][:, h * 2 * P : (h + 1) * 2 * P].rearrange("p (g r) -> p g r", r=TEAM),
+                    turned[b, h][:].rearrange("p (g r) -> p g r", r=TEAM),
+                    1.0,
+                    coef[b][:, h * GH : (h + 1) * GH].unsqueeze(2).to_broadcast([P, GH, TEAM]),
+                    ALU.subtract,
+                    ALU.mult,
+                )
+        for b, c0, c1 in ((0, 0, J), (1, 0, J // 2), (1, J // 2, J)):
+            nc.vector.tensor_tensor(res[b][:, c0:c1], old_sb[b][:, c0:c1], grad[b][:, c0:c1], ALU.subtract)
+            nc.sync.dma_start(out[b * P : (b + 1) * P, c0:c1], res[b][:, c0:c1])

from contextlib import ExitStack

import concourse.mybir as mybir
from concourse.masks import make_identity

D, T, U, I, J, G = 512, 1024, 1024, 256, 512, 128
FLOPS = 2 * D * I * J

F32 = mybir.dt.float32
BF16 = mybir.dt.bfloat16
I32 = mybir.dt.int32
U32 = mybir.dt.uint32
U16 = mybir.dt.uint16
U8 = mybir.dt.uint8
FP8X4 = mybir.dt.float8_e4m3fn_x4
ALU = mybir.AluOpType
ACT = mybir.ActivationFunctionType

P = 128
PACK = 4
TEAM = J // G
BLOCKS = I // P
JB = J // P


def tile_attend_bpairteams_kernel(tc, taba, tabb_words, tabb_scales, stake, bias, old, offs, offs2, out):
    nc = tc.nc
    with ExitStack() as ctx:
        keep = ctx.enter_context(tc.tile_pool(name="keep", bufs=1))
        psum = ctx.enter_context(tc.psum_pool(name="psum", bufs=1))

        a_rows = taba.rearrange("(p t) n -> p t n", t=PACK)
        a_planes = [keep.tile([P, T], F32, name=f"a_plane{t}", align_bytes=64) for t in range(PACK)]
        both = range(BLOCKS)

        offs2_sb = keep.tile([P, J // 16], U16, name="offs2_sb")
        nc.sync.dma_start(offs2_sb[:], offs2)
        nc.sync.dma_start(a_planes[0][:], a_rows[:, 0, :])
        offs_sb = keep.tile([P, I // 16], U16, name="offs_sb")
        nc.sync.dma_start(offs_sb[:], offs)

        b_scale_table = keep.tile([P, U], U8, name="b_scale_table", align_bytes=64)
        for q in range(4):
            rows = tabb_scales[0, 4 * q : 4 * q + 4, :].bitcast(I32)
            nc.scalar.dma_start(
                b_scale_table[32 * q : 32 * q + 32, :].bitcast(I32),
                rows.unsqueeze(0).to_broadcast([8, 4, U // 4]),
            )
        for t in range(1, PACK):
            nc.sync.dma_start(a_planes[t][:], a_rows[:, t, :])
        b_word_table = keep.tile([P, U], I32, name="b_word_table", align_bytes=64)
        nc.sync.dma_start(b_word_table[:], tabb_words[0].rearrange("p n t -> p (n t)").bitcast(I32))

        bias_rows = keep.tile([P, P], F32, name="bias_rows")
        nc.gpsimd.memset(bias_rows[:], 0.0)
        nc.scalar.dma_start(bias_rows[0:JB, :], bias.rearrange("o (c p) -> (o c) p", p=P))
        stake_sb = keep.tile([P, BLOCKS, G], F32, name="stake_sb")
        nc.sync.dma_start(stake_sb[:], stake.rearrange("(b p) g -> p b g", p=P))
        old_sb = []
        for b in both:
            o = keep.tile([P, J], F32, name=f"old{b}")
            nc.sync.dma_start(o[:], old[b * P : (b + 1) * P, :])
            old_sb.append(o)

        ident = keep.tile([P, P], F32, name="ident")
        make_identity(nc, ident[:])
        bias_turned = psum.tile([P, 2 * P], F32, name="bias_turned", tag="turned11")
        nc.tensor.transpose(bias_turned[:, 0:P], bias_rows[:], ident[:])
        bias_sb = keep.tile([P, JB], F32, name="bias_sb")
        nc.vector.tensor_copy(bias_sb[:], bias_turned[:, 0:JB])

        b_scales = keep.tile([P, J], U8, name="b_scales", align_bytes=64)
        nc.vector.tensor_copy(b_scales[:], b_scale_table[:].indirect(offs2_sb[:]))

        grouped = keep.tile([P, I, PACK], BF16, name="grouped", align_bytes=64)
        for t in range(PACK):
            nc.vector.tensor_copy(grouped[:, :, t], a_planes[t][:].indirect(offs_sb[:]))
        a_words = keep.tile([P, I], U32, name="a_words", align_bytes=64)
        a_scales = keep.tile([P, I], U8, name="a_scales", align_bytes=64)
        nc.vector.quantize_mx(out=a_words[:].bitcast(FP8X4), scales=a_scales[:], in_=grouped[:].rearrange("p n t -> p (n t)"))

        cols = P // 16
        turned = {}
        for b in both:
            for h in range(2):
                turned[b, h] = psum.tile([P, 2 * P], F32, name=f"turned{b}{h}", tag=f"turned{b}{h}")
        wins = []
        for c in range(JB):
            b_words = keep.tile([P, P], U32, name=f"b_words{c}", align_bytes=64)
            nc.vector.tensor_copy(b_words[:], b_word_table[:].bitcast(U32).indirect(offs2_sb[:, c * cols : (c + 1) * cols]))
            scores = psum.tile([P, I], F32, name=f"scores{c}")
            nc.tensor.matmul_mx(
                out=scores[:],
                lhsT=b_words[:].bitcast(FP8X4),
                lhsT_scale=b_scales[:, c * P : (c + 1) * P],
                rhs=a_words[:].bitcast(FP8X4),
                rhs_scale=a_scales[:],
                start=True,
                stop=True,
            )
            win = keep.tile([P, I], F32, name=f"win{c}")
            nc.scalar.activation(win[:], scores[:], ACT.Sigmoid, bias=bias_sb[:, c : c + 1], scale=1.0)
            wins.append(win)
        for c in range(JB):
            h, e = divmod(c, 2)
            for b in both:
                nc.tensor.transpose(turned[b, h][:, e * P : (e + 1) * P], wins[c][:, b * P : (b + 1) * P], ident[:])

        def tiles(name, shape):
            return [keep.tile(shape, F32, name=f"{name}{b}") for b in both]

        chance = tiles("chance", [P, G])
        squared = tiles("squared", [P, G])
        staked = tiles("staked", [P, G])
        inv = tiles("inv", [P, G])
        coef = tiles("coef", [P, G])
        grad = tiles("grad", [P, J])
        res = tiles("res", [P, J])
        GH = G // 2
        for h in range(2):
            for b in both:
                nc.vector.tensor_reduce(
                    chance[b][:, h * GH : (h + 1) * GH],
                    turned[b, h][:].rearrange("p (g r) -> p g r", r=TEAM),
                    mybir.AxisListType.X,
                    ALU.mult,
                )
        for b in both:
            nc.vector.scalar_tensor_tensor(squared[b][:], chance[b][:], 2.0, chance[b][:], ALU.add, ALU.mult)
        for b in both:
            nc.vector.tensor_tensor(staked[b][:], chance[b][:], stake_sb[:, b, :], ALU.mult)
        for b in both:
            nc.scalar.activation(inv[b][:], squared[b][:], ACT.Abs_reciprocal_sqrt, bias=1.0, scale=1.0)
        for b in both:
            nc.vector.tensor_tensor(coef[b][:], staked[b][:], inv[b][:], ALU.mult)
        for b in both:
            for h in range(2):
                nc.vector.scalar_tensor_tensor(
                    grad[b][:, h * 2 * P : (h + 1) * 2 * P].rearrange("p (g r) -> p g r", r=TEAM),
                    turned[b, h][:].rearrange("p (g r) -> p g r", r=TEAM),
                    1.0,
                    coef[b][:, h * GH : (h + 1) * GH].unsqueeze(2).to_broadcast([P, GH, TEAM]),
                    ALU.subtract,
                    ALU.mult,
                )
        for b, c0, c1 in ((0, 0, J), (1, 0, J // 2), (1, J // 2, J)):
            nc.vector.tensor_tensor(res[b][:, c0:c1], old_sb[b][:, c0:c1], grad[b][:, c0:c1], ALU.subtract)
            nc.sync.dma_start(out[b * P : (b + 1) * P, c0:c1], res[b][:, c0:c1])
